import numpy as np
import ml_dtypes


def mxq(x, axis, fmt="e4m3"):
    dtype, down = {"e4m3": (ml_dtypes.float8_e4m3fn, 7), "e5m2": (ml_dtypes.float8_e5m2, 14)}[fmt]
    v = np.moveaxis(np.asarray(x, np.float32).astype(ml_dtypes.bfloat16).astype(np.float64), axis, -1)
    blocks = v.reshape(v.shape[:-1] + (-1, 32))
    amax = np.abs(blocks).max(-1, keepdims=True)
    byte = np.maximum(np.where(amax > 0, np.frexp(amax)[1] - 1 + 127, 0) - down, 1)
    scale = np.exp2(byte - 127.0)
    codes = (blocks / scale).astype(np.float32).astype(dtype).astype(np.float64)
    return np.moveaxis((codes * scale).reshape(v.shape), -1, axis)


WIDE = False


def mx_kscale(k):
    if not WIDE:
        return np.ones(k)
    levels = np.array([18, -18])
    if k % 512:
        return np.exp2(np.random.permutation(np.resize(levels, k // 32))).repeat(32)
    a = np.empty((k // 512, 16))
    for p in range(k // 512):
        a[p, :8] = np.random.permutation(np.resize(levels, 8))
        for g in range(8):
            far = levels[np.abs(levels - a[p, g]) >= 10]
            a[p, g + 8] = far[np.random.randint(len(far))]
    return np.exp2(a.ravel()).repeat(32)


def f64(x):
    return np.asarray(x).astype(np.float64)


def striped(idx):
    return np.tile(np.asarray(idx).reshape(-1, 16).T, (8, 1)).astype(np.uint16)


def unstriped(offs):
    return offs[:16].T.reshape(-1).astype(np.int64)

def planes(y):
    n, m = y.shape
    v = y.astype(np.float32).astype(ml_dtypes.bfloat16).astype(np.float64).reshape(n // 32, 32, m)
    top = np.abs(v).max(1)
    byte = np.clip(np.where(top > 0, np.frexp(top)[1] - 1 + 127 - 7, 1), 1, 254)
    codes = (v * np.exp2(127.0 - byte)[:, None, :]).reshape(n, m).astype(np.float32).astype(ml_dtypes.float8_e4m3fn).view(np.uint8)
    words = codes.reshape(n // 512, 128, 4, m).transpose(0, 1, 3, 2)
    return np.ascontiguousarray(words), np.ascontiguousarray(byte.astype(np.uint8).reshape(n // 512, 16, m))


N, C, D, R = 512, 4096, 512, 512


def eight(codes):
    return np.concatenate([codes[h].reshape(-1, 16).T for h in range(8)]).astype(np.uint16)


def uneight(offs):
    return np.stack([offs[16 * h:16 * h + 16].T.reshape(-1) for h in range(8)]).astype(np.int64)


def setup_inputs():
    n = np.random.standard_normal
    s = mx_kscale(D)[:, None]
    u = mx_kscale(N)
    grid = lambda x: np.round(x * 32) / 32
    return {
        "xT": (n((D, R)) * (1.0 / np.sqrt(D)) * s).astype(np.float32),
        "cb": (grid(n((D, C))) / s).astype(np.float32),
        "norm": np.tile(np.random.randint(32, 129, N) / 64.0 / u, (128, 1)).astype(np.float32),
        "ts": np.tile(np.random.uniform(0.5, 1.5, N) * u, (128, 1)).astype(np.float32),
        "y": n((R, N)).astype(np.float32),
        "wt": (np.random.uniform(0.5, 1.5, (R, 1)) * 1.0 / np.sqrt(N)).astype(np.float32),
        "offs": eight(np.random.randint(0, C, (8, N))),
    }


def reference(xT, cb, norm, ts, y, wt, offs):
    code = uneight(offs)
    k = np.concatenate([f64(cb)[64 * h:64 * h + 64][:, code[h]] for h in range(8)]) * f64(norm)[:1]
    a = f64(ts)[:1] * (mxq(f64(xT), 0, "e4m3").T @ mxq(k, 0, "e4m3"))
    g = f64(wt) * (a - f64(y))
    h = f64(ts)[:1] * g
    out_0 = mxq(h, 1, "e5m2") @ mxq(k, 1, "e4m3").T
    return (out_0,) + planes(out_0)

@@ -1,0 +1,210 @@
+from contextlib import ExitStack
+
+import concourse.mybir as mybir
+from concourse.masks import make_identity
+
+N, C, D, R = 512, 4096, 512, 512
+FLOPS = 2 * 2 * N * D * R
+
+F32 = mybir.dt.float32
+BF16 = mybir.dt.bfloat16
+I32 = mybir.dt.int32
+U32 = mybir.dt.uint32
+U16 = mybir.dt.uint16
+U8 = mybir.dt.uint8
+E4M3 = mybir.dt.float8_e4m3fn_x4
+E5M2 = mybir.dt.float8_e5m2_x4
+MULT = mybir.AluOpType.mult
+COPY = mybir.ActivationFunctionType.Copy
+
+P = 128
+PACK = 4
+HALF = N // 2
+
+
+def tile_attend_gpq_pl_sq_x_kernel(tc, xT, cb, norm, ts, y, wt, offs, out_0, out_1, out_2):
+    nc = tc.nc
+    with ExitStack() as ctx:
+        keep = ctx.enter_context(tc.tile_pool(name="keep", bufs=1))
+        psum = ctx.enter_context(tc.psum_pool(name="psum", bufs=1))
+
+        def sbuf(name, shape, dtype):
+            return keep.tile(shape, dtype, name=name, align_bytes=64)
+
+        def quantize(codes, scales, values, fmt):
+            nc.vector.quantize_mx(out=codes.bitcast(fmt), scales=scales, in_=values)
+
+        offsets = keep.tile([P, N // 16], U16, name="offsets")
+        nc.sync.dma_start(offsets[:], offs)
+        norm_col = sbuf("norm_col", [P, PACK], F32)
+        nc.sync.dma_start(norm_col[:], norm[0:1, :].rearrange("o (p c) -> p (o c)", c=PACK))
+        x_raw = sbuf("x_raw", [P, PACK, R], F32)
+        nc.sync.dma_start(x_raw[:], xT.rearrange("(p e) r -> p e r", e=PACK))
+        books = [sbuf(f"book{e}", [P, C], F32) for e in range(PACK)]
+        cb_planes = cb.rearrange("(p e) c -> e p c", e=PACK)
+        nc.sync.dma_start(books[0][:], cb_planes[0])
+        ts_col = sbuf("ts_col", [P, PACK], F32)
+        nc.sync.dma_start(ts_col[:], ts[0:1, :].rearrange("o (p c) -> p (o c)", c=PACK))
+        wt_col = sbuf("wt_col", [P, PACK], F32)
+        nc.sync.dma_start(wt_col[:], wt.rearrange("(p j) o -> p (j o)", j=PACK))
+        for e in range(1, PACK):
+            nc.sync.dma_start(books[e][:], cb_planes[e])
+        y_rows = y.rearrange("(m j) n -> j m n", j=PACK)
+        y_raw = [sbuf(f"y_raw{j}", [P, N], F32) for j in range(PACK)]
+        for j in range(PACK):
+            nc.sync.dma_start(y_raw[j][:], y_rows[j])
+
+        ident = sbuf("ident", [P, P], F32)
+        make_identity(nc, ident[:])
+
+        def spread(col):
+            bank = psum.tile([P, PACK, P], F32, name="score", bufs=3)
+            for c in range(PACK):
+                nc.tensor.transpose(bank[:, c, :], col[:, c : c + 1].to_broadcast([P, P]), ident[:])
+            return bank
+
+        norm_row = sbuf("norm_row", [P, N], F32)
+        nc.scalar.copy(norm_row[:].rearrange("m (p c) -> m p c", c=PACK), spread(norm_col)[:].rearrange("m c p -> m p c"))
+        ts_row = sbuf("ts_row", [P, PACK, P], F32)
+        nc.scalar.copy(ts_row[:], spread(ts_col)[:])
+        neg_wt = sbuf("neg_wt", [P, PACK], F32)
+        nc.vector.tensor_scalar(neg_wt[:], wt_col[:], -1.0, None, MULT)
+
+        x_bf = sbuf("x_bf", [P, R * PACK], BF16)
+        nc.vector.tensor_copy(
+            x_bf[:].rearrange("p (j m e) -> p m e j", j=PACK, e=PACK),
+            x_raw[:].rearrange("p e (m j) -> p m e j", j=PACK),
+        )
+        x_codes = sbuf("x_codes", [P, R], U32)
+        x_scales = sbuf("x_scales", [P, R], U8)
+        quantize(x_codes[:], x_scales[:], x_bf[:], E4M3)
+
+        k_f32 = [sbuf(f"k_f32_{e}", [P, N], F32) for e in range(PACK)]
+        k_bf = [sbuf(f"k_bf{h}", [P, HALF, PACK], BF16) for h in range(2)]
+        kd_codes = sbuf("kd_codes", [P, N], U32)
+        kd_scales = sbuf("kd_scales", [P, N], U8)
+        kn_codes = sbuf("kn_codes", [P, D], U32)
+        kn_scales = sbuf("kn_scales", [P, D], U8)
+
+        def gather(e, h):
+            cols = slice(h * HALF, (h + 1) * HALF)
+            lists = offsets[:, h * HALF // 16 : (h + 1) * HALF // 16]
+            nc.vector.tensor_tensor(k_f32[e][:, cols], books[e][:].indirect(lists), norm_row[:, cols], MULT)
+            if h == 0:
+                nc.scalar.copy(k_bf[h][:, :, e], k_f32[e][:, cols])
+            else:
+                nc.vector.tensor_copy(k_bf[h][:, :, e], k_f32[e][:, cols])
+
+        def turn_k(e):
+            bank = psum.tile([P, PACK, P], F32, name="turn", bufs=1)
+            for t in range(PACK):
+                nc.tensor.transpose(bank[:, t, :], k_f32[e][:, t::PACK], ident[:])
+            turned = sbuf(f"k_turned{e}", [P, P, PACK], BF16)
+            nc.scalar.copy(turned[:], bank[:].rearrange("s t p -> s p t"))
+            return turned
+
+        def quantize_turned(e, turned):
+            cols = slice(e * P, (e + 1) * P)
+            quantize(kn_codes[:, cols], kn_scales[:, cols], turned[:].rearrange("s p t -> s (p t)"), E4M3)
+
+        for e in range(PACK):
+            for h in range(2):
+                gather(e, h)
+            if e < PACK - 1:
+                quantize_turned(e, turn_k(e))
+        for h in range(2):
+            cols = slice(h * HALF, (h + 1) * HALF)
+            quantize(kd_codes[:, cols], kd_scales[:, cols], k_bf[h][:].rearrange("p n e -> p (n e)"), E4M3)
+
+        grads = []
+        for j in range(PACK):
+            y_dealt = sbuf(f"y_dealt{j}", [P, PACK, P], F32)
+            nc.scalar.activation(
+                y_dealt[:].rearrange("m t s -> m s t"),
+                y_raw[j][:].rearrange("m (s t) -> m s t", t=PACK),
+                COPY,
+                scale=neg_wt[:, j : j + 1],
+            )
+            bank = psum.tile([P, PACK, P], F32, name=f"grad{j}", bufs=1)
+            for t in range(PACK):
+                nc.tensor.matmul(bank[:, t, :], y_dealt[:, t, :], ident[:], start=(t == 0), stop=False, is_transpose=True)
+            grads.append(bank)
+
+        weighted = []
+        for j in range(PACK):
+            rows = slice(j * P, (j + 1) * P)
+            score = psum.tile([P, N], F32, name="score", bufs=3)
+            nc.tensor.matmul_mx(
+                out=score[:],
+                lhsT=x_codes[:, rows].bitcast(E4M3),
+                lhsT_scale=x_scales[:, rows],
+                rhs=kd_codes[:].bitcast(E4M3),
+                rhs_scale=kd_scales[:],
+                start=True,
+                stop=True,
+            )
+            wa = sbuf(f"weighted{j}", [P, PACK, P], F32)
+            nc.vector.scalar_tensor_tensor(
+                wa[:], score[:].rearrange("m (s t) -> m t s", t=PACK), wt_col[:, j : j + 1], ts_row[:], MULT, MULT
+            )
+            weighted.append(wa)
+        last_turned = turn_k(PACK - 1)
+        for j in range(PACK):
+            for t in range(PACK):
+                nc.tensor.matmul(
+                    grads[j][:, t, :], weighted[j][:, t, :], ident[:], start=False, stop=(t == PACK - 1), is_transpose=True
+                )
+        quantize_turned(PACK - 1, last_turned)
+
+        result = sbuf("result", [P, PACK, D], F32)
+        out_rows = out_0.rearrange("(m j) d -> j m d", j=PACK)
+        h_bf = [sbuf(f"h_bf{j}", [P, P, PACK], BF16) for j in range(PACK)]
+
+        def scale_h(j):
+            nc.vector.tensor_tensor(
+                h_bf[j][:], grads[j][:].rearrange("s t m -> s m t"), ts_col[:].unsqueeze(1).to_broadcast([P, P, PACK]), MULT
+            )
+
+        def second_product(j):
+            h_codes = sbuf(f"h_codes{j}", [P, P], U32)
+            h_scales = sbuf(f"h_scales{j}", [P, P], U8)
+            quantize(h_codes[:], h_scales[:], h_bf[j][:].rearrange("s m t -> s (m t)"), E5M2)
+            bank = psum.tile([P, D], F32, name=f"grad{j}", bufs=1)
+            nc.tensor.matmul_mx(
+                out=bank[:],
+                lhsT=h_codes[:].bitcast(E5M2),
+                lhsT_scale=h_scales[:],
+                rhs=kn_codes[:].bitcast(E4M3),
+                rhs_scale=kn_scales[:],
+                start=True,
+                stop=True,
+            )
+            nc.scalar.copy(result[:, j, :].rearrange("m (p e) -> m p e", e=PACK), bank[:].rearrange("m (e p) -> m p e", e=PACK))
+            nc.sync.dma_start(out_rows[j], result[:, j, :])
+
+        scale_h(0)
+        for j in range(1, PACK):
+            scale_h(j)
+            second_product(j - 1)
+        second_product(PACK - 1)
+
+        o_codes = sbuf("o_codes", [P, D], U32)
+        o_scales = sbuf("o_scales", [P, D], U8)
+        o_bf = [sbuf(f"o_bf{h}", [P, HALF * PACK], BF16) for h in range(2)]
+        words = out_1.rearrange("o p d b -> p (o d b)").bitcast(I32)
+        for h in range(2):
+            cols = slice(h * HALF, (h + 1) * HALF)
+            dst = o_bf[h][:].rearrange("m (c i j) -> m c j i", i=4, j=PACK)
+            src = result[:, :, cols].rearrange("m j (c i) -> m c j i", i=4)
+            if h == 0:
+                nc.vector.tensor_copy(dst, src)
+            else:
+                nc.scalar.copy(dst, src)
+        for h in range(2):
+            cols = slice(h * HALF, (h + 1) * HALF)
+            quantize(o_codes[:, cols], o_scales[:, cols], o_bf[h][:], E4M3)
+            nc.sync.dma_start(words[:, cols], o_codes[:, cols].bitcast(I32))
+        scale_rows = out_2.rearrange("o f d -> (o f) d").bitcast(I32)
+        for q in range(4):
+            queue = nc.scalar if q % 2 else nc.sync
+            queue.dma_start(scale_rows[4 * q : 4 * q + 4, :], o_scales[32 * q : 32 * q + 4, :].bitcast(I32))

@@ -28,27 +28,29 @@ def tile_attend_gpq_pl_sq_x_kernel(tc, xT, cb, norm, ts, y, wt, offs, out_0, out
         keep = ctx.enter_context(tc.tile_pool(name="keep", bufs=1))
         psum = ctx.enter_context(tc.psum_pool(name="psum", bufs=1))
 
-        def sbuf(name, shape, dtype):
-            return keep.tile(shape, dtype, name=name, align_bytes=64)
+        def sbuf(name, shape, dtype, slot=None):
+            return keep.tile(shape, dtype, name=name, tag=slot or name, align_bytes=64)
 
         def quantize(codes, scales, values, fmt):
             nc.vector.quantize_mx(out=codes.bitcast(fmt), scales=scales, in_=values)
 
+        books = [sbuf(f"book{e}", [P, C], F32) for e in range(PACK)]
+        cb_planes = cb.rearrange("(p e) c -> e p c", e=PACK)
+        nc.sync.dma_start(books[0][:], cb_planes[0])
         offsets = keep.tile([P, N // 16], U16, name="offsets")
         nc.sync.dma_start(offsets[:], offs)
         norm_col = sbuf("norm_col", [P, PACK], F32)
         nc.sync.dma_start(norm_col[:], norm[0:1, :].rearrange("o (p c) -> p (o c)", c=PACK))
-        x_raw = sbuf("x_raw", [P, PACK, R], F32)
-        nc.sync.dma_start(x_raw[:], xT.rearrange("(p e) r -> p e r", e=PACK))
-        books = [sbuf(f"book{e}", [P, C], F32) for e in range(PACK)]
-        cb_planes = cb.rearrange("(p e) c -> e p c", e=PACK)
-        nc.sync.dma_start(books[0][:], cb_planes[0])
         ts_col = sbuf("ts_col", [P, PACK], F32)
         nc.sync.dma_start(ts_col[:], ts[0:1, :].rearrange("o (p c) -> p (o c)", c=PACK))
         wt_col = sbuf("wt_col", [P, PACK], F32)
         nc.sync.dma_start(wt_col[:], wt.rearrange("(p j) o -> p (j o)", j=PACK))
         for e in range(1, PACK):
             nc.sync.dma_start(books[e][:], cb_planes[e])
+        x_raw = sbuf("x_raw", [P, PACK * R], F32)
+        x_halves = xT.rearrange("(p e) (b r) -> b p e r", e=PACK, b=2)
+        for b in range(2):
+            nc.sync.dma_start(x_raw[:].rearrange("p (b e r) -> p b e r", b=2, e=PACK)[:, b], x_halves[b])
         y_rows = y.rearrange("(m j) n -> j m n", j=PACK)
         y_raw = [sbuf(f"y_raw{j}", [P, N], F32) for j in range(PACK)]
         for j in range(PACK):
@@ -58,7 +60,7 @@ def tile_attend_gpq_pl_sq_x_kernel(tc, xT, cb, norm, ts, y, wt, offs, out_0, out
         make_identity(nc, ident[:])
 
         def spread(col):
-            bank = psum.tile([P, PACK, P], F32, name="score", bufs=3)
+            bank = psum.tile([P, PACK, P], F32, name="turn", bufs=1)
             for c in range(PACK):
                 nc.tensor.transpose(bank[:, c, :], col[:, c : c + 1].to_broadcast([P, P]), ident[:])
             return bank
@@ -70,19 +72,8 @@ def tile_attend_gpq_pl_sq_x_kernel(tc, xT, cb, norm, ts, y, wt, offs, out_0, out
         neg_wt = sbuf("neg_wt", [P, PACK], F32)
         nc.vector.tensor_scalar(neg_wt[:], wt_col[:], -1.0, None, MULT)
 
-        x_bf = sbuf("x_bf", [P, R * PACK], BF16)
-        nc.vector.tensor_copy(
-            x_bf[:].rearrange("p (j m e) -> p m e j", j=PACK, e=PACK),
-            x_raw[:].rearrange("p e (m j) -> p m e j", j=PACK),
-        )
-        x_codes = sbuf("x_codes", [P, R], U32)
-        x_scales = sbuf("x_scales", [P, R], U8)
-        quantize(x_codes[:], x_scales[:], x_bf[:], E4M3)
-
         k_f32 = [sbuf(f"k_f32_{e}", [P, N], F32) for e in range(PACK)]
         k_bf = [sbuf(f"k_bf{h}", [P, HALF, PACK], BF16) for h in range(2)]
-        kd_codes = sbuf("kd_codes", [P, N], U32)
-        kd_scales = sbuf("kd_scales", [P, N], U8)
         kn_codes = sbuf("kn_codes", [P, D], U32)
         kn_scales = sbuf("kn_scales", [P, D], U8)
 
@@ -90,31 +81,94 @@ def tile_attend_gpq_pl_sq_x_kernel(tc, xT, cb, norm, ts, y, wt, offs, out_0, out
             cols = slice(h * HALF, (h + 1) * HALF)
             lists = offsets[:, h * HALF // 16 : (h + 1) * HALF // 16]
             nc.vector.tensor_tensor(k_f32[e][:, cols], books[e][:].indirect(lists), norm_row[:, cols], MULT)
-            if h == 0:
-                nc.scalar.copy(k_bf[h][:, :, e], k_f32[e][:, cols])
-            else:
-                nc.vector.tensor_copy(k_bf[h][:, :, e], k_f32[e][:, cols])
+
+        def weave(e, h):
+            copy = nc.vector.tensor_copy if h else nc.scalar.copy
+            copy(k_bf[h][:, :, e], k_f32[e][:, h * HALF : (h + 1) * HALF])
 
         def turn_k(e):
             bank = psum.tile([P, PACK, P], F32, name="turn", bufs=1)
             for t in range(PACK):
                 nc.tensor.transpose(bank[:, t, :], k_f32[e][:, t::PACK], ident[:])
-            turned = sbuf(f"k_turned{e}", [P, P, PACK], BF16)
-            nc.scalar.copy(turned[:], bank[:].rearrange("s t p -> s p t"))
+            return bank
+
+        def round_turned(copy, e, bank, slot=None):
+            turned = sbuf(f"k_turned{e}", [P, P, PACK], BF16, slot)
+            copy(turned[:], bank[:].rearrange("s t p -> s p t"))
             return turned
 
         def quantize_turned(e, turned):
-            cols = slice(e * P, (e + 1) * P)
-            quantize(kn_codes[:, cols], kn_scales[:, cols], turned[:].rearrange("s p t -> s (p t)"), E4M3)
+            for v in range(2):
+                cols = slice(v * HALF + e * 64, v * HALF + (e + 1) * 64)
+                values = turned[:, v * 64 : (v + 1) * 64, :].rearrange("s p t -> s (p t)")
+                quantize(kn_codes[:, cols], kn_scales[:, cols], values, E4M3)
 
         for e in range(PACK):
             for h in range(2):
                 gather(e, h)
+            for h in range(2):
+                weave(e, h)
             if e < PACK - 1:
-                quantize_turned(e, turn_k(e))
+                quantize_turned(e, round_turned(nc.scalar.copy, e, turn_k(e)))
+        last_bank = turn_k(PACK - 1)
+
+        kd_codes = sbuf("kd_codes", [P, N], U32)
+        kd_scales = sbuf("kd_scales", [P, N], U8)
         for h in range(2):
             cols = slice(h * HALF, (h + 1) * HALF)
             quantize(kd_codes[:, cols], kd_scales[:, cols], k_bf[h][:].rearrange("p n e -> p (n e)"), E4M3)
+
+        x_bf = [sbuf(f"x_bf{a}", [P, 2, P * PACK], BF16) for a in range(2)]
+
+        x_pairs = x_raw[:].rearrange("p (b e m a j) -> p a b m e j", b=2, e=PACK, a=2, j=2)
+        x_woven = [t[:].rearrange("p j (b m e) -> p b m e j", b=2, e=PACK) for t in x_bf]
+        for b in range(2):
+            nc.scalar.copy(x_woven[0][:, b], x_pairs[:, 0, b])
+        nc.scalar.copy(x_woven[1], x_pairs[:, 1])
+        x_codes = [sbuf(f"x_codes{j}", [P, P], U32) for j in range(PACK)]
+        x_scales = [sbuf(f"x_scales{j}", [P, P], U8) for j in range(PACK)]
+        weighted = [sbuf(f"weighted{j}", [P, PACK, P], F32) for j in range(PACK)]
+
+        def quantize_x(j):
+            quantize(x_codes[j][:], x_scales[j][:], x_bf[j // 2][:, j % 2, :], E4M3)
+
+        def first_product(j, bank_name, lo, hi):
+            score = psum.tile([P, N], F32, name=bank_name, bufs=1)
+            nc.tensor.matmul_mx(
+                out=score[:, lo:hi],
+                lhsT=x_codes[j][:].bitcast(E4M3),
+                lhsT_scale=x_scales[j][:],
+                rhs=kd_codes[:, lo:hi].bitcast(E4M3),
+                rhs_scale=kd_scales[:, lo:hi],
+                start=True,
+                stop=True,
+            )
+            return score[:, lo:hi]
+
+        def weigh(j, score, lo, hi):
+            s_cols = slice(lo // PACK, hi // PACK)
+            nc.vector.scalar_tensor_tensor(
+                weighted[j][:, :, s_cols],
+                score.rearrange("m (s t) -> m t s", t=PACK),
+                wt_col[:, j : j + 1],
+                ts_row[:, :, s_cols],
+                MULT,
+                MULT,
+            )
+
+        quantize_x(0)
+        quantize_x(1)
+        early = first_product(0, "early", 0, HALF)
+        late = first_product(0, "grad1", HALF, N)
+        score = first_product(1, "grad0", 0, N)
+        weigh(0, early, 0, HALF)
+        weigh(0, late, HALF, N)
+        scores = [score]
+        for j in (2, 3):
+            quantize_x(j)
+            scores.append(first_product(j, f"grad{j}", 0, N))
+        for j in (1, 2, 3):
+            weigh(j, scores[j - 1], 0, N)
 
         grads = []
         for j in range(PACK):
@@ -127,33 +181,14 @@ def tile_attend_gpq_pl_sq_x_kernel(tc, xT, cb, norm, ts, y, wt, offs, out_0, out
             )
             bank = psum.tile([P, PACK, P], F32, name=f"grad{j}", bufs=1)
             for t in range(PACK):
-                nc.tensor.matmul(bank[:, t, :], y_dealt[:, t, :], ident[:], start=(t == 0), stop=False, is_transpose=True)
-            grads.append(bank)
-
-        weighted = []
-        for j in range(PACK):
-            rows = slice(j * P, (j + 1) * P)
-            score = psum.tile([P, N], F32, name="score", bufs=3)
-            nc.tensor.matmul_mx(
-                out=score[:],
-                lhsT=x_codes[:, rows].bitcast(E4M3),
-                lhsT_scale=x_scales[:, rows],
-                rhs=kd_codes[:].bitcast(E4M3),
-                rhs_scale=kd_scales[:],
-                start=True,
-                stop=True,
-            )
-            wa = sbuf(f"weighted{j}", [P, PACK, P], F32)
-            nc.vector.scalar_tensor_tensor(
-                wa[:], score[:].rearrange("m (s t) -> m t s", t=PACK), wt_col[:, j : j + 1], ts_row[:], MULT, MULT
-            )
-            weighted.append(wa)
-        last_turned = turn_k(PACK - 1)
-        for j in range(PACK):
+                nc.tensor.matmul(bank[:, t, :], weighted[j][:, t, :], ident[:], start=(t == 0), stop=False, is_transpose=True)
             for t in range(PACK):
                 nc.tensor.matmul(
-                    grads[j][:, t, :], weighted[j][:, t, :], ident[:], start=False, stop=(t == PACK - 1), is_transpose=True
+                    bank[:, t, :], y_dealt[:, t, :], ident[:], start=False, stop=(t == PACK - 1), is_transpose=True
                 )
+            grads.append(bank)
+            if j == 1:
+                last_turned = round_turned(nc.scalar.copy, PACK - 1, last_bank, "y_raw1")
         quantize_turned(PACK - 1, last_turned)
 
         result = sbuf("result", [P, PACK, D], F32)
@@ -169,40 +204,52 @@ def tile_attend_gpq_pl_sq_x_kernel(tc, xT, cb, norm, ts, y, wt, offs, out_0, out
             h_codes = sbuf(f"h_codes{j}", [P, P], U32)
             h_scales = sbuf(f"h_scales{j}", [P, P], U8)
             quantize(h_codes[:], h_scales[:], h_bf[j][:].rearrange("s m t -> s (m t)"), E5M2)
-            bank = psum.tile([P, D], F32, name=f"grad{j}", bufs=1)
-            nc.tensor.matmul_mx(
-                out=bank[:],
-                lhsT=h_codes[:].bitcast(E5M2),
-                lhsT_scale=h_scales[:],
-                rhs=kn_codes[:].bitcast(E4M3),
-                rhs_scale=kn_scales[:],
-                start=True,
-                stop=True,
-            )
-            nc.scalar.copy(result[:, j, :].rearrange("m (p e) -> m p e", e=PACK), bank[:].rearrange("m (e p) -> m p e", e=PACK))
+            parts = [(f"grad{j}", 0, D)] if j < PACK - 1 else [("early", 0, HALF), (f"grad{j}", HALF, D)]
+            for bank_name, lo, hi in parts:
+                bank = psum.tile([P, D], F32, name=bank_name, bufs=1)
+                nc.tensor.matmul_mx(
+                    out=bank[:, lo:hi],
+                    lhsT=h_codes[:].bitcast(E5M2),
+                    lhsT_scale=h_scales[:],
+                    rhs=kn_codes[:, lo:hi].bitcast(E4M3),
+                    rhs_scale=kn_scales[:, lo:hi],
+                    start=True,
+                    stop=True,
+                )
+                nc.scalar.copy(
+                    result[:, j, lo:hi].rearrange("m (v p e) -> m v p e", p=64, e=PACK),
+                    bank[:, lo:hi].rearrange("m (v e p) -> m v p e", p=64, e=PACK),
+                )
             nc.sync.dma_start(out_rows[j], result[:, j, :])
 
         scale_h(0)
-        for j in range(1, PACK):
-            scale_h(j)
-            second_product(j - 1)
-        second_product(PACK - 1)
+        scale_h(1)
+        second_product(0)
+        scale_h(2)
+        second_product(1)
+        second_product(2)
+        scale_h(3)
+        second_product(3)
 
         o_codes = sbuf("o_codes", [P, D], U32)
         o_scales = sbuf("o_scales", [P, D], U8)
-        o_bf = [sbuf(f"o_bf{h}", [P, HALF * PACK], BF16) for h in range(2)]
+        o_bf = sbuf("o_bf", [P, D * PACK], BF16, "h_bf3")
         words = out_1.rearrange("o p d b -> p (o d b)").bitcast(I32)
+
+        def weave_out(copy, pair, lo, hi):
+            tiles = slice(2 * pair, 2 * pair + 2)
+            copy(
+                o_bf[:].rearrange("m (d j) -> m d j", j=PACK)[:, lo:hi, tiles].rearrange("m (c i) j -> m c j i", i=4),
+                result[:, tiles, lo:hi].rearrange("m j (c i) -> m c j i", i=4),
+            )
+
+        weave_out(nc.vector.tensor_copy, 0, 0, D)
+        weave_out(nc.vector.tensor_copy, 1, 0, HALF)
+        weave_out(nc.vector.tensor_copy, 1, HALF, HALF + P)
+        weave_out(nc.scalar.copy, 1, HALF + P, D)
         for h in range(2):
             cols = slice(h * HALF, (h + 1) * HALF)
-            dst = o_bf[h][:].rearrange("m (c i j) -> m c j i", i=4, j=PACK)
-            src = result[:, :, cols].rearrange("m j (c i) -> m c j i", i=4)
-            if h == 0:
-                nc.vector.tensor_copy(dst, src)
-            else:
-                nc.scalar.copy(dst, src)
-        for h in range(2):
-            cols = slice(h * HALF, (h + 1) * HALF)
-            quantize(o_codes[:, cols], o_scales[:, cols], o_bf[h][:], E4M3)
+            quantize(o_codes[:, cols], o_scales[:, cols], o_bf[:, h * HALF * PACK : (h + 1) * HALF * PACK], E4M3)
             nc.sync.dma_start(words[:, cols], o_codes[:, cols].bitcast(I32))
         scale_rows = out_2.rearrange("o f d -> (o f) d").bitcast(I32)
         for q in range(4):

@@ -19,7 +19,11 @@ COPY = mybir.ActivationFunctionType.Copy
 
 P = 128
 PACK = 4
-HALF = N // 2
+LAST = PACK - 1
+HALF = 256
+LIST_ROWS = 16
+LINE = 4
+QUADRANT = 32
 
 
 def tile_attend_gpq_pl_sq_x_kernel(tc, xT, cb, norm, ts, y, wt, offs, out_0, out_1, out_2):
@@ -37,20 +41,20 @@ def tile_attend_gpq_pl_sq_x_kernel(tc, xT, cb, norm, ts, y, wt, offs, out_0, out
         books = [sbuf(f"book{e}", [P, C], F32) for e in range(PACK)]
         cb_planes = cb.rearrange("(p e) c -> e p c", e=PACK)
         nc.sync.dma_start(books[0][:], cb_planes[0])
-        offsets = keep.tile([P, N // 16], U16, name="offsets")
+        offsets = keep.tile([P, N // LIST_ROWS], U16, name="offsets")
         nc.sync.dma_start(offsets[:], offs)
         norm_col = sbuf("norm_col", [P, PACK], F32)
-        nc.sync.dma_start(norm_col[:], norm[0:1, :].rearrange("o (p c) -> p (o c)", c=PACK))
+        nc.sync.dma_start(norm_col[:], norm[0:1, :].rearrange("o (s t) -> s (o t)", t=PACK))
         ts_col = sbuf("ts_col", [P, PACK], F32)
-        nc.sync.dma_start(ts_col[:], ts[0:1, :].rearrange("o (p c) -> p (o c)", c=PACK))
+        nc.sync.dma_start(ts_col[:], ts[0:1, :].rearrange("o (s t) -> s (o t)", t=PACK))
         wt_col = sbuf("wt_col", [P, PACK], F32)
-        nc.sync.dma_start(wt_col[:], wt.rearrange("(p j) o -> p (j o)", j=PACK))
+        nc.sync.dma_start(wt_col[:], wt.rearrange("(m j) o -> m (j o)", j=PACK))
         for e in range(1, PACK):
             nc.sync.dma_start(books[e][:], cb_planes[e])
-        x_raw = sbuf("x_raw", [P, PACK * R], F32)
+        x_raw = [sbuf(f"x_raw{b}", [P, PACK, HALF], F32) for b in range(2)]
         x_halves = xT.rearrange("(p e) (b r) -> b p e r", e=PACK, b=2)
         for b in range(2):
-            nc.sync.dma_start(x_raw[:].rearrange("p (b e r) -> p b e r", b=2, e=PACK)[:, b], x_halves[b])
+            nc.sync.dma_start(x_raw[b][:], x_halves[b])
         y_rows = y.rearrange("(m j) n -> j m n", j=PACK)
         y_raw = [sbuf(f"y_raw{j}", [P, N], F32) for j in range(PACK)]
         for j in range(PACK):
@@ -61,30 +65,30 @@ def tile_attend_gpq_pl_sq_x_kernel(tc, xT, cb, norm, ts, y, wt, offs, out_0, out
 
         def spread(col):
             bank = psum.tile([P, PACK, P], F32, name="turn", bufs=1)
-            for c in range(PACK):
-                nc.tensor.transpose(bank[:, c, :], col[:, c : c + 1].to_broadcast([P, P]), ident[:])
+            for t in range(PACK):
+                nc.tensor.transpose(bank[:, t, :], col[:, t : t + 1].to_broadcast([P, P]), ident[:])
             return bank
 
         norm_row = sbuf("norm_row", [P, N], F32)
-        nc.scalar.copy(norm_row[:].rearrange("m (p c) -> m p c", c=PACK), spread(norm_col)[:].rearrange("m c p -> m p c"))
+        nc.scalar.copy(norm_row[:].rearrange("m (s t) -> m s t", t=PACK), spread(norm_col)[:].rearrange("m t s -> m s t"))
         ts_row = sbuf("ts_row", [P, PACK, P], F32)
         nc.scalar.copy(ts_row[:], spread(ts_col)[:])
         neg_wt = sbuf("neg_wt", [P, PACK], F32)
         nc.vector.tensor_scalar(neg_wt[:], wt_col[:], -1.0, None, MULT)
 
         k_f32 = [sbuf(f"k_f32_{e}", [P, N], F32) for e in range(PACK)]
-        k_bf = [sbuf(f"k_bf{h}", [P, HALF, PACK], BF16) for h in range(2)]
+        k_woven = [sbuf(f"k_woven{u}", [P, HALF, PACK], BF16) for u in range(2)]
         kn_codes = sbuf("kn_codes", [P, D], U32)
         kn_scales = sbuf("kn_scales", [P, D], U8)
 
-        def gather(e, h):
-            cols = slice(h * HALF, (h + 1) * HALF)
-            lists = offsets[:, h * HALF // 16 : (h + 1) * HALF // 16]
+        def gather(e, u):
+            cols = slice(u * HALF, (u + 1) * HALF)
+            lists = offsets[:, u * HALF // LIST_ROWS : (u + 1) * HALF // LIST_ROWS]
             nc.vector.tensor_tensor(k_f32[e][:, cols], books[e][:].indirect(lists), norm_row[:, cols], MULT)
 
-        def weave(e, h):
-            copy = nc.vector.tensor_copy if h else nc.scalar.copy
-            copy(k_bf[h][:, :, e], k_f32[e][:, h * HALF : (h + 1) * HALF])
+        def weave_k(e, u):
+            copy = nc.vector.tensor_copy if u else nc.scalar.copy
+            copy(k_woven[u][:, :, e], k_f32[e][:, u * HALF : (u + 1) * HALF])
 
         def turn_k(e):
             bank = psum.tile([P, PACK, P], F32, name="turn", bufs=1)
@@ -92,119 +96,102 @@ def tile_attend_gpq_pl_sq_x_kernel(tc, xT, cb, norm, ts, y, wt, offs, out_0, out
                 nc.tensor.transpose(bank[:, t, :], k_f32[e][:, t::PACK], ident[:])
             return bank
 
-        def round_turned(copy, e, bank, slot=None):
+        def weave_turned(e, bank, slot=None):
             turned = sbuf(f"k_turned{e}", [P, P, PACK], BF16, slot)
-            copy(turned[:], bank[:].rearrange("s t p -> s p t"))
+            nc.scalar.copy(turned[:], bank[:].rearrange("s t p -> s p t"))
             return turned
 
         def quantize_turned(e, turned):
             for v in range(2):
-                cols = slice(v * HALF + e * 64, v * HALF + (e + 1) * 64)
-                values = turned[:, v * 64 : (v + 1) * 64, :].rearrange("s p t -> s (p t)")
+                cols = slice(v * HALF + e * P // 2, v * HALF + (e + 1) * P // 2)
+                values = turned[:, v * P // 2 : (v + 1) * P // 2, :].rearrange("s p t -> s (p t)")
                 quantize(kn_codes[:, cols], kn_scales[:, cols], values, E4M3)
 
         for e in range(PACK):
-            for h in range(2):
-                gather(e, h)
-            for h in range(2):
-                weave(e, h)
-            if e < PACK - 1:
-                quantize_turned(e, round_turned(nc.scalar.copy, e, turn_k(e)))
-        last_bank = turn_k(PACK - 1)
+            for u in range(2):
+                gather(e, u)
+            for u in range(2):
+                weave_k(e, u)
+            if e < LAST:
+                quantize_turned(e, weave_turned(e, turn_k(e)))
+        last_plane_bank = turn_k(LAST)
 
-        kd_codes = sbuf("kd_codes", [P, N], U32)
+        x_woven = sbuf("x_woven", [P, R * PACK], BF16)
+        for b, copy in enumerate((nc.scalar.copy, nc.vector.tensor_copy)):
+            copy(
+                x_woven[:].rearrange("p (j b m e) -> p b m e j", j=PACK, b=2, e=PACK)[:, b],
+                x_raw[b][:].rearrange("p e (m j) -> p m e j", j=PACK),
+            )
+
+        kd_codes = sbuf("kd_codes", [P, N], U32, "x_raw1")
         kd_scales = sbuf("kd_scales", [P, N], U8)
-        for h in range(2):
-            cols = slice(h * HALF, (h + 1) * HALF)
-            quantize(kd_codes[:, cols], kd_scales[:, cols], k_bf[h][:].rearrange("p n e -> p (n e)"), E4M3)
+        for u in range(2):
+            cols = slice(u * HALF, (u + 1) * HALF)
+            quantize(kd_codes[:, cols], kd_scales[:, cols], k_woven[u][:].rearrange("p n e -> p (n e)"), E4M3)
 
-        x_bf = [sbuf(f"x_bf{a}", [P, 2, P * PACK], BF16) for a in range(2)]
-
-        x_pairs = x_raw[:].rearrange("p (b e m a j) -> p a b m e j", b=2, e=PACK, a=2, j=2)
-        x_woven = [t[:].rearrange("p j (b m e) -> p b m e j", b=2, e=PACK) for t in x_bf]
-        for b in range(2):
-            nc.scalar.copy(x_woven[0][:, b], x_pairs[:, 0, b])
-        nc.scalar.copy(x_woven[1], x_pairs[:, 1])
         x_codes = [sbuf(f"x_codes{j}", [P, P], U32) for j in range(PACK)]
         x_scales = [sbuf(f"x_scales{j}", [P, P], U8) for j in range(PACK)]
         weighted = [sbuf(f"weighted{j}", [P, PACK, P], F32) for j in range(PACK)]
-
-        def quantize_x(j):
-            quantize(x_codes[j][:], x_scales[j][:], x_bf[j // 2][:, j % 2, :], E4M3)
-
-        def first_product(j, bank_name, lo, hi):
-            score = psum.tile([P, N], F32, name=bank_name, bufs=1)
+        scores = []
+        for j in range(PACK):
+            quantize(x_codes[j][:], x_scales[j][:], x_woven[:, j * P * PACK : (j + 1) * P * PACK], E4M3)
+            score = psum.tile([P, N], F32, name=f"tile{j}", bufs=1)
             nc.tensor.matmul_mx(
-                out=score[:, lo:hi],
+                out=score[:],
                 lhsT=x_codes[j][:].bitcast(E4M3),
                 lhsT_scale=x_scales[j][:],
-                rhs=kd_codes[:, lo:hi].bitcast(E4M3),
-                rhs_scale=kd_scales[:, lo:hi],
+                rhs=kd_codes[:].bitcast(E4M3),
+                rhs_scale=kd_scales[:],
                 start=True,
                 stop=True,
             )
-            return score[:, lo:hi]
-
-        def weigh(j, score, lo, hi):
-            s_cols = slice(lo // PACK, hi // PACK)
+            scores.append(score)
+        for j in range(PACK):
             nc.vector.scalar_tensor_tensor(
-                weighted[j][:, :, s_cols],
-                score.rearrange("m (s t) -> m t s", t=PACK),
+                weighted[j][:],
+                scores[j][:].rearrange("m (s t) -> m t s", t=PACK),
                 wt_col[:, j : j + 1],
-                ts_row[:, :, s_cols],
+                ts_row[:],
                 MULT,
                 MULT,
             )
 
-        quantize_x(0)
-        quantize_x(1)
-        early = first_product(0, "early", 0, HALF)
-        late = first_product(0, "grad1", HALF, N)
-        score = first_product(1, "grad0", 0, N)
-        weigh(0, early, 0, HALF)
-        weigh(0, late, HALF, N)
-        scores = [score]
-        for j in (2, 3):
-            quantize_x(j)
-            scores.append(first_product(j, f"grad{j}", 0, N))
-        for j in (1, 2, 3):
-            weigh(j, scores[j - 1], 0, N)
-
         grads = []
         for j in range(PACK):
-            y_dealt = sbuf(f"y_dealt{j}", [P, PACK, P], F32)
+            neg_wy = sbuf(f"neg_wy{j}", [P, PACK, P], F32)
             nc.scalar.activation(
-                y_dealt[:].rearrange("m t s -> m s t"),
+                neg_wy[:].rearrange("m t s -> m s t"),
                 y_raw[j][:].rearrange("m (s t) -> m s t", t=PACK),
                 COPY,
                 scale=neg_wt[:, j : j + 1],
             )
-            bank = psum.tile([P, PACK, P], F32, name=f"grad{j}", bufs=1)
+            grad = psum.tile([P, PACK, P], F32, name=f"tile{j}", bufs=1)
             for t in range(PACK):
-                nc.tensor.matmul(bank[:, t, :], weighted[j][:, t, :], ident[:], start=(t == 0), stop=False, is_transpose=True)
+                nc.tensor.matmul(grad[:, t, :], weighted[j][:, t, :], ident[:], start=(t == 0), stop=False, is_transpose=True)
             for t in range(PACK):
-                nc.tensor.matmul(
-                    bank[:, t, :], y_dealt[:, t, :], ident[:], start=False, stop=(t == PACK - 1), is_transpose=True
-                )
-            grads.append(bank)
+                nc.tensor.matmul(grad[:, t, :], neg_wy[:, t, :], ident[:], start=False, stop=(t == LAST), is_transpose=True)
+            grads.append(grad)
             if j == 1:
-                last_turned = round_turned(nc.scalar.copy, PACK - 1, last_bank, "y_raw1")
-        quantize_turned(PACK - 1, last_turned)
+                last_turned = weave_turned(LAST, last_plane_bank, "y_raw1")
+        quantize_turned(LAST, last_turned)
 
         result = sbuf("result", [P, PACK, D], F32)
         out_rows = out_0.rearrange("(m j) d -> j m d", j=PACK)
-        h_bf = [sbuf(f"h_bf{j}", [P, P, PACK], BF16) for j in range(PACK)]
+        h_woven = [sbuf(f"h_woven{j}", [P, P, PACK], BF16) for j in range(PACK)]
 
         def scale_h(j):
             nc.vector.tensor_tensor(
-                h_bf[j][:], grads[j][:].rearrange("s t m -> s m t"), ts_col[:].unsqueeze(1).to_broadcast([P, P, PACK]), MULT
+                h_woven[j][:],
+                grads[j][:].rearrange("s t m -> s m t"),
+                ts_col[:].unsqueeze(1).to_broadcast([P, P, PACK]),
+                MULT,
             )
 
         def second_product(j):
             h_codes = sbuf(f"h_codes{j}", [P, P], U32)
             h_scales = sbuf(f"h_scales{j}", [P, P], U8)
-            quantize(h_codes[:], h_scales[:], h_bf[j][:].rearrange("s m t -> s (m t)"), E5M2)
-            parts = [(f"grad{j}", 0, D)] if j < PACK - 1 else [("early", 0, HALF), (f"grad{j}", HALF, D)]
+            quantize(h_codes[:], h_scales[:], h_woven[j][:].rearrange("s m t -> s (m t)"), E5M2)
+            parts = [(f"tile{j}", 0, D)] if j < LAST else [("last_half", 0, HALF), (f"tile{j}", HALF, D)]
             for bank_name, lo, hi in parts:
                 bank = psum.tile([P, D], F32, name=bank_name, bufs=1)
                 nc.tensor.matmul_mx(
@@ -217,8 +204,8 @@ def tile_attend_gpq_pl_sq_x_kernel(tc, xT, cb, norm, ts, y, wt, offs, out_0, out
                     stop=True,
                 )
                 nc.scalar.copy(
-                    result[:, j, lo:hi].rearrange("m (v p e) -> m v p e", p=64, e=PACK),
-                    bank[:, lo:hi].rearrange("m (v e p) -> m v p e", p=64, e=PACK),
+                    result[:, j, lo:hi].rearrange("m (v i e) -> m v i e", i=P // 2, e=PACK),
+                    bank[:, lo:hi].rearrange("m (v e i) -> m v i e", i=P // 2, e=PACK),
                 )
             nc.sync.dma_start(out_rows[j], result[:, j, :])
 
@@ -228,30 +215,30 @@ def tile_attend_gpq_pl_sq_x_kernel(tc, xT, cb, norm, ts, y, wt, offs, out_0, out
         scale_h(2)
         second_product(1)
         second_product(2)
-        scale_h(3)
-        second_product(3)
+        scale_h(LAST)
+        second_product(LAST)
 
-        o_codes = sbuf("o_codes", [P, D], U32)
-        o_scales = sbuf("o_scales", [P, D], U8)
-        o_bf = sbuf("o_bf", [P, D * PACK], BF16, "h_bf3")
-        words = out_1.rearrange("o p d b -> p (o d b)").bitcast(I32)
+        out_codes = sbuf("out_codes", [P, D], U32)
+        out_scales = sbuf("out_scales", [P, D], U8)
+        out_woven = sbuf("out_woven", [P, D * PACK], BF16, f"h_woven{LAST}")
+        words = out_1.rearrange("o m d j -> m (o d j)").bitcast(I32)
 
         def weave_out(copy, pair, lo, hi):
             tiles = slice(2 * pair, 2 * pair + 2)
             copy(
-                o_bf[:].rearrange("m (d j) -> m d j", j=PACK)[:, lo:hi, tiles].rearrange("m (c i) j -> m c j i", i=4),
-                result[:, tiles, lo:hi].rearrange("m j (c i) -> m c j i", i=4),
+                out_woven[:].rearrange("m (d j) -> m d j", j=PACK)[:, lo:hi, tiles].rearrange("m (c i) j -> m c j i", i=LINE),
+                result[:, tiles, lo:hi].rearrange("m j (c i) -> m c j i", i=LINE),
             )
 
         weave_out(nc.vector.tensor_copy, 0, 0, D)
         weave_out(nc.vector.tensor_copy, 1, 0, HALF)
-        weave_out(nc.vector.tensor_copy, 1, HALF, HALF + P)
-        weave_out(nc.scalar.copy, 1, HALF + P, D)
-        for h in range(2):
-            cols = slice(h * HALF, (h + 1) * HALF)
-            quantize(o_codes[:, cols], o_scales[:, cols], o_bf[:, h * HALF * PACK : (h + 1) * HALF * PACK], E4M3)
-            nc.sync.dma_start(words[:, cols], o_codes[:, cols].bitcast(I32))
+        weave_out(nc.vector.tensor_copy, 1, HALF, 3 * D // 4)
+        weave_out(nc.scalar.copy, 1, 3 * D // 4, D)
+        for v in range(2):
+            cols = slice(v * HALF, (v + 1) * HALF)
+            quantize(out_codes[:, cols], out_scales[:, cols], out_woven[:, v * HALF * PACK : (v + 1) * HALF * PACK], E4M3)
+            nc.sync.dma_start(words[:, cols], out_codes[:, cols].bitcast(I32))
         scale_rows = out_2.rearrange("o f d -> (o f) d").bitcast(I32)
-        for q in range(4):
+        for q in range(P // QUADRANT):
             queue = nc.scalar if q % 2 else nc.sync
-            queue.dma_start(scale_rows[4 * q : 4 * q + 4, :], o_scales[32 * q : 32 * q + 4, :].bitcast(I32))
+            queue.dma_start(scale_rows[4 * q : 4 * q + 4, :], out_scales[QUADRANT * q : QUADRANT * q + 4, :].bitcast(I32))

from contextlib import ExitStack

import concourse.mybir as mybir
from concourse.masks import make_identity

N, C, D, R = 512, 4096, 512, 512
FLOPS = 2 * 2 * N * D * R

F32 = mybir.dt.float32
BF16 = mybir.dt.bfloat16
I32 = mybir.dt.int32
U32 = mybir.dt.uint32
U16 = mybir.dt.uint16
U8 = mybir.dt.uint8
E4M3 = mybir.dt.float8_e4m3fn_x4
E5M2 = mybir.dt.float8_e5m2_x4
MULT = mybir.AluOpType.mult
COPY = mybir.ActivationFunctionType.Copy

P = 128
PACK = 4
LAST = PACK - 1
HALF = 256
LIST_ROWS = 16
LINE = 4
QUADRANT = 32


def tile_attend_gpq_pl_sq_x_kernel(tc, xT, cb, norm, ts, y, wt, offs, out_0, out_1, out_2):
    nc = tc.nc
    with ExitStack() as ctx:
        keep = ctx.enter_context(tc.tile_pool(name="keep", bufs=1))
        psum = ctx.enter_context(tc.psum_pool(name="psum", bufs=1))

        def sbuf(name, shape, dtype, slot=None):
            return keep.tile(shape, dtype, name=name, tag=slot or name, align_bytes=64)

        def quantize(codes, scales, values, fmt):
            nc.vector.quantize_mx(out=codes.bitcast(fmt), scales=scales, in_=values)

        books = [sbuf(f"book{e}", [P, C], F32) for e in range(PACK)]
        cb_planes = cb.rearrange("(p e) c -> e p c", e=PACK)
        nc.sync.dma_start(books[0][:], cb_planes[0])
        offsets = keep.tile([P, N // LIST_ROWS], U16, name="offsets")
        nc.sync.dma_start(offsets[:], offs)
        norm_col = sbuf("norm_col", [P, PACK], F32)
        nc.sync.dma_start(norm_col[:], norm[0:1, :].rearrange("o (s t) -> s (o t)", t=PACK))
        ts_col = sbuf("ts_col", [P, PACK], F32)
        nc.sync.dma_start(ts_col[:], ts[0:1, :].rearrange("o (s t) -> s (o t)", t=PACK))
        wt_col = sbuf("wt_col", [P, PACK], F32)
        nc.sync.dma_start(wt_col[:], wt.rearrange("(m j) o -> m (j o)", j=PACK))
        for e in range(1, PACK):
            nc.sync.dma_start(books[e][:], cb_planes[e])
        x_raw = [sbuf(f"x_raw{b}", [P, PACK, HALF], F32) for b in range(2)]
        x_halves = xT.rearrange("(p e) (b r) -> b p e r", e=PACK, b=2)
        for b in range(2):
            nc.sync.dma_start(x_raw[b][:], x_halves[b])
        y_rows = y.rearrange("(m j) n -> j m n", j=PACK)
        y_raw = [sbuf(f"y_raw{j}", [P, N], F32) for j in range(PACK)]
        for j in range(PACK):
            nc.sync.dma_start(y_raw[j][:], y_rows[j])

        ident = sbuf("ident", [P, P], F32)
        make_identity(nc, ident[:])

        def spread(col):
            bank = psum.tile([P, PACK, P], F32, name="turn", bufs=1)
            for t in range(PACK):
                nc.tensor.transpose(bank[:, t, :], col[:, t : t + 1].to_broadcast([P, P]), ident[:])
            return bank

        norm_row = sbuf("norm_row", [P, N], F32)
        nc.scalar.copy(norm_row[:].rearrange("m (s t) -> m s t", t=PACK), spread(norm_col)[:].rearrange("m t s -> m s t"))
        ts_row = sbuf("ts_row", [P, PACK, P], F32)
        nc.scalar.copy(ts_row[:], spread(ts_col)[:])
        neg_wt = sbuf("neg_wt", [P, PACK], F32)
        nc.vector.tensor_scalar(neg_wt[:], wt_col[:], -1.0, None, MULT)

        k_f32 = [sbuf(f"k_f32_{e}", [P, N], F32) for e in range(PACK)]
        k_woven = [sbuf(f"k_woven{u}", [P, HALF, PACK], BF16) for u in range(2)]
        kn_codes = sbuf("kn_codes", [P, D], U32)
        kn_scales = sbuf("kn_scales", [P, D], U8)

        def gather(e, u):
            cols = slice(u * HALF, (u + 1) * HALF)
            lists = offsets[:, u * HALF // LIST_ROWS : (u + 1) * HALF // LIST_ROWS]
            nc.vector.tensor_tensor(k_f32[e][:, cols], books[e][:].indirect(lists), norm_row[:, cols], MULT)

        def weave_k(e, u):
            copy = nc.vector.tensor_copy if u else nc.scalar.copy
            copy(k_woven[u][:, :, e], k_f32[e][:, u * HALF : (u + 1) * HALF])

        def turn_k(e):
            bank = psum.tile([P, PACK, P], F32, name="turn", bufs=1)
            for t in range(PACK):
                nc.tensor.transpose(bank[:, t, :], k_f32[e][:, t::PACK], ident[:])
            return bank

        def weave_turned(e, bank, slot=None):
            turned = sbuf(f"k_turned{e}", [P, P, PACK], BF16, slot)
            nc.scalar.copy(turned[:], bank[:].rearrange("s t p -> s p t"))
            return turned

        def quantize_turned(e, turned):
            for v in range(2):
                cols = slice(v * HALF + e * P // 2, v * HALF + (e + 1) * P // 2)
                values = turned[:, v * P // 2 : (v + 1) * P // 2, :].rearrange("s p t -> s (p t)")
                quantize(kn_codes[:, cols], kn_scales[:, cols], values, E4M3)

        for e in range(PACK):
            for u in range(2):
                gather(e, u)
            for u in range(2):
                weave_k(e, u)
            if e < LAST:
                quantize_turned(e, weave_turned(e, turn_k(e)))
        last_plane_bank = turn_k(LAST)

        x_woven = sbuf("x_woven", [P, R * PACK], BF16)
        for b, copy in enumerate((nc.scalar.copy, nc.vector.tensor_copy)):
            copy(
                x_woven[:].rearrange("p (j b m e) -> p b m e j", j=PACK, b=2, e=PACK)[:, b],
                x_raw[b][:].rearrange("p e (m j) -> p m e j", j=PACK),
            )

        kd_codes = sbuf("kd_codes", [P, N], U32, "x_raw1")
        kd_scales = sbuf("kd_scales", [P, N], U8)
        for u in range(2):
            cols = slice(u * HALF, (u + 1) * HALF)
            quantize(kd_codes[:, cols], kd_scales[:, cols], k_woven[u][:].rearrange("p n e -> p (n e)"), E4M3)

        x_codes = [sbuf(f"x_codes{j}", [P, P], U32) for j in range(PACK)]
        x_scales = [sbuf(f"x_scales{j}", [P, P], U8) for j in range(PACK)]
        weighted = [sbuf(f"weighted{j}", [P, PACK, P], F32) for j in range(PACK)]
        scores = []
        for j in range(PACK):
            quantize(x_codes[j][:], x_scales[j][:], x_woven[:, j * P * PACK : (j + 1) * P * PACK], E4M3)
            score = psum.tile([P, N], F32, name=f"tile{j}", bufs=1)
            nc.tensor.matmul_mx(
                out=score[:],
                lhsT=x_codes[j][:].bitcast(E4M3),
                lhsT_scale=x_scales[j][:],
                rhs=kd_codes[:].bitcast(E4M3),
                rhs_scale=kd_scales[:],
                start=True,
                stop=True,
            )
            scores.append(score)
        for j in range(PACK):
            nc.vector.scalar_tensor_tensor(
                weighted[j][:],
                scores[j][:].rearrange("m (s t) -> m t s", t=PACK),
                wt_col[:, j : j + 1],
                ts_row[:],
                MULT,
                MULT,
            )

        grads = []
        for j in range(PACK):
            neg_wy = sbuf(f"neg_wy{j}", [P, PACK, P], F32)
            nc.scalar.activation(
                neg_wy[:].rearrange("m t s -> m s t"),
                y_raw[j][:].rearrange("m (s t) -> m s t", t=PACK),
                COPY,
                scale=neg_wt[:, j : j + 1],
            )
            grad = psum.tile([P, PACK, P], F32, name=f"tile{j}", bufs=1)
            for t in range(PACK):
                nc.tensor.matmul(grad[:, t, :], weighted[j][:, t, :], ident[:], start=(t == 0), stop=False, is_transpose=True)
            for t in range(PACK):
                nc.tensor.matmul(grad[:, t, :], neg_wy[:, t, :], ident[:], start=False, stop=(t == LAST), is_transpose=True)
            grads.append(grad)
            if j == 1:
                last_turned = weave_turned(LAST, last_plane_bank, "y_raw1")
        quantize_turned(LAST, last_turned)

        result = sbuf("result", [P, PACK, D], F32)
        out_rows = out_0.rearrange("(m j) d -> j m d", j=PACK)
        h_woven = [sbuf(f"h_woven{j}", [P, P, PACK], BF16) for j in range(PACK)]

        def scale_h(j):
            nc.vector.tensor_tensor(
                h_woven[j][:],
                grads[j][:].rearrange("s t m -> s m t"),
                ts_col[:].unsqueeze(1).to_broadcast([P, P, PACK]),
                MULT,
            )

        def second_product(j):
            h_codes = sbuf(f"h_codes{j}", [P, P], U32)
            h_scales = sbuf(f"h_scales{j}", [P, P], U8)
            quantize(h_codes[:], h_scales[:], h_woven[j][:].rearrange("s m t -> s (m t)"), E5M2)
            parts = [(f"tile{j}", 0, D)] if j < LAST else [("last_half", 0, HALF), (f"tile{j}", HALF, D)]
            for bank_name, lo, hi in parts:
                bank = psum.tile([P, D], F32, name=bank_name, bufs=1)
                nc.tensor.matmul_mx(
                    out=bank[:, lo:hi],
                    lhsT=h_codes[:].bitcast(E5M2),
                    lhsT_scale=h_scales[:],
                    rhs=kn_codes[:, lo:hi].bitcast(E4M3),
                    rhs_scale=kn_scales[:, lo:hi],
                    start=True,
                    stop=True,
                )
                nc.scalar.copy(
                    result[:, j, lo:hi].rearrange("m (v i e) -> m v i e", i=P // 2, e=PACK),
                    bank[:, lo:hi].rearrange("m (v e i) -> m v i e", i=P // 2, e=PACK),
                )
            nc.sync.dma_start(out_rows[j], result[:, j, :])

        scale_h(0)
        scale_h(1)
        second_product(0)
        scale_h(2)
        second_product(1)
        second_product(2)
        scale_h(LAST)
        second_product(LAST)

        out_codes = sbuf("out_codes", [P, D], U32)
        out_scales = sbuf("out_scales", [P, D], U8)
        out_woven = sbuf("out_woven", [P, D * PACK], BF16, f"h_woven{LAST}")
        words = out_1.rearrange("o m d j -> m (o d j)").bitcast(I32)

        def weave_out(copy, pair, lo, hi):
            tiles = slice(2 * pair, 2 * pair + 2)
            copy(
                out_woven[:].rearrange("m (d j) -> m d j", j=PACK)[:, lo:hi, tiles].rearrange("m (c i) j -> m c j i", i=LINE),
                result[:, tiles, lo:hi].rearrange("m j (c i) -> m c j i", i=LINE),
            )

        weave_out(nc.vector.tensor_copy, 0, 0, D)
        weave_out(nc.vector.tensor_copy, 1, 0, HALF)
        weave_out(nc.vector.tensor_copy, 1, HALF, 3 * D // 4)
        weave_out(nc.scalar.copy, 1, 3 * D // 4, D)
        for v in range(2):
            cols = slice(v * HALF, (v + 1) * HALF)
            quantize(out_codes[:, cols], out_scales[:, cols], out_woven[:, v * HALF * PACK : (v + 1) * HALF * PACK], E4M3)
            nc.sync.dma_start(words[:, cols], out_codes[:, cols].bitcast(I32))
        scale_rows = out_2.rearrange("o f d -> (o f) d").bitcast(I32)
        for q in range(P // QUADRANT):
            queue = nc.scalar if q % 2 else nc.sync
            queue.dma_start(scale_rows[4 * q : 4 * q + 4, :], out_scales[QUADRANT * q : QUADRANT * q + 4, :].bitcast(I32))
